import numpy as np
import ml_dtypes


def mxq(x, axis, fmt="e4m3"):
    dtype, down = {"e4m3": (ml_dtypes.float8_e4m3fn, 7), "e5m2": (ml_dtypes.float8_e5m2, 14)}[fmt]
    v = np.moveaxis(np.asarray(x, np.float32).astype(ml_dtypes.bfloat16).astype(np.float64), axis, -1)
    blocks = v.reshape(v.shape[:-1] + (-1, 32))
    amax = np.abs(blocks).max(-1, keepdims=True)
    byte = np.maximum(np.where(amax > 0, np.frexp(amax)[1] - 1 + 127, 0) - down, 1)
    scale = np.exp2(byte - 127.0)
    codes = (blocks / scale).astype(np.float32).astype(dtype).astype(np.float64)
    return np.moveaxis((codes * scale).reshape(v.shape), -1, axis)


WIDE = False


def mx_kscale(k):
    if not WIDE:
        return np.ones(k)
    levels = np.array([10, -10, 5, -5, 0])
    if k % 512:
        return np.exp2(np.random.permutation(np.resize(levels, k // 32))).repeat(32)
    a = np.empty((k // 512, 16))
    for p in range(k // 512):
        a[p, :8] = np.random.permutation(np.resize(levels, 8))
        for g in range(8):
            far = levels[np.abs(levels - a[p, g]) >= 10]
            a[p, g + 8] = far[np.random.randint(len(far))]
    return np.exp2(a.ravel()).repeat(32)


def f64(x):
    return np.asarray(x).astype(np.float64)


def striped(idx):
    return np.tile(idx.reshape(-1, 16).T, (8, 1)).astype(np.uint16)


def unstriped(offs):
    return offs[:16].T.reshape(-1).astype(np.int64)


E2M1 = np.array([0.0, 0.5, 1.0, 1.5, 2.0, 3.0, 4.0, 6.0, -0.0, -0.5, -1.0, -1.5, -2.0, -3.0, -4.0, -6.0])


def pack_weight(w, fmt):
    k, n = w.shape
    w = f64(np.asarray(w, np.float32).astype(ml_dtypes.bfloat16)).reshape(k // 32, 32, n)
    amax = np.abs(w).max(1)
    if fmt == "e4m3":
        byte = np.frexp(amax)[1] - 1 + 127 - 7
    else:
        mant, ex = np.frexp(amax / 6.0)
        byte = np.where(mant > 0.5, ex, ex - 1) + 127
    byte = np.clip(np.where(amax > 0, byte, 1), 1, 254)
    scaled = (w * np.exp2(127.0 - byte)[:, None, :]).reshape(k, n).astype(np.float32)
    by_word = np.ascontiguousarray(scaled.reshape(k // 512, 128, 4, n).transpose(0, 1, 3, 2))
    if fmt == "e4m3":
        words = by_word.astype(ml_dtypes.float8_e4m3fn).view(np.uint8)
    else:
        c = by_word.astype(ml_dtypes.float4_e2m1fn).view(np.uint8) & 0xF
        words = (c[..., 0::2] | (c[..., 1::2] << 4)).reshape(k // 512, 128, 2 * n)
    return np.ascontiguousarray(words), np.ascontiguousarray(byte.astype(np.uint8).reshape(k // 512, 16, n))


def unpack_weight(words, scales, fmt):
    g, _, n = scales.shape
    words = np.ascontiguousarray(words).reshape(g, 128, n, -1)
    if fmt == "e4m3":
        vals = words.view(ml_dtypes.float8_e4m3fn).astype(np.float64)
    else:
        nib = np.empty((g, 128, n, 4), np.uint8)
        nib[..., 0::2] = words & 0xF
        nib[..., 1::2] = words >> 4
        vals = E2M1[nib]
    vals = vals * np.repeat(np.exp2(scales.astype(np.float64) - 127.0), 8, axis=1)[..., None]
    return vals.transpose(0, 1, 3, 2).reshape(g * 512, n)


def gelu(v):
    return 0.5 * v * (1.0 + np.tanh(np.sqrt(2.0 / np.pi) * (v + 0.044715 * v**3)))


def bf(x):
    return np.asarray(x, np.float32).astype(ml_dtypes.bfloat16)


def planes(Y):
    n, m = Y.shape
    b = f64(bf(Y)).reshape(n // 32, 32, m)
    amax = np.abs(b).max(1)
    byte = np.clip(np.where(amax > 0, np.frexp(amax)[1] - 1 + 127 - 7, 1), 1, 254)
    codes = (b * np.exp2(127.0 - byte)[:, None, :]).reshape(n, m).astype(np.float32).astype(ml_dtypes.float8_e4m3fn).view(np.uint8)
    words = codes.reshape(n // 512, 128, 4, m).transpose(0, 1, 3, 2)
    return np.ascontiguousarray(words), np.ascontiguousarray(byte.astype(np.uint8).reshape(n // 512, 16, m))


K, H, N, T, S, P, P2 = 1024, 1024, 512, 4096, 1024, 512, 256

def setup_inputs():
    n = np.random.standard_normal
    s = mx_kscale(K)[:, None]
    u = mx_kscale(H)[:, None]
    e = np.exp(0.8 * n(N))
    d = {}
    d["tab_words"], d["tab_scales"] = pack_weight(n((K, T)) * s, "e4m3")
    d["offs"] = striped(np.random.permutation(T)[:S])
    d["pos1"] = striped(np.random.permutation(S)[:P])
    d["pos2"] = striped(np.random.permutation(P)[:P2])
    d["w1"] = (0.37 * n((K, H)) / s / K ** 0.5).astype(np.float32)
    d["phase"] = np.random.uniform(-1.2, 1.2, H).astype(np.float32)
    d["gain"] = (np.sign(n(H)) * np.exp(0.3 * n(H)) * u[:, 0]).astype(np.float32)
    d["w2_words"], d["w2_scales"] = pack_weight(n((H, H)) / u * u.T / H ** 0.5, "e4m3")
    d["w3"] = (n((H, N)) / u / H ** 0.5).astype(np.float32)
    d["w4_words"], d["w4_scales"] = pack_weight(n((H, N)) / u * e / H ** 0.5, "e2m1")
    d["base"] = (0.6 * n((N, P2)) * e[:, None]).astype(np.float32)
    return d

def reference(tab_words, tab_scales, offs, pos1, pos2, w1, phase, gain, w2_words, w2_scales, w3, w4_words, w4_scales, base):
    v = unpack_weight(tab_words, tab_scales, "e4m3")[:, unstriped(offs)]
    a = (mxq(f64(w1), 0, "e4m3").T @ v) + f64(phase)[:, None]
    h = f64(gain)[:, None] * np.cos(a)
    x1 = h[:, unstriped(pos1)]
    w2 = unpack_weight(w2_words, w2_scales, "e4m3")
    st = w2.T @ mxq(x1, 0, "e4m3")
    x2 = x1 + 0.9 * np.minimum(st, x1)
    x3 = mxq(x2[:, unstriped(pos2)], 0, "e4m3")
    f = mxq(f64(w3), 0, "e4m3").T @ x3
    w4 = unpack_weight(w4_words, w4_scales, "e2m1")
    l = w4.T @ x3
    y = np.tanh(f) * l + f64(base)
    words, scales = planes(y)
    return y, words, scales

@@ -1,0 +1,393 @@
+import math
+from contextlib import ExitStack
+
+import concourse.mybir as mybir
+
+K, H, N, T, S, P1, P2 = 1024, 1024, 512, 4096, 1024, 512, 256
+FLOPS = 2 * K * H * S + 2 * H * H * P1 + 2 * 2 * H * N * P2
+
+F32 = mybir.dt.float32
+BF16 = mybir.dt.bfloat16
+I32 = mybir.dt.int32
+U32 = mybir.dt.uint32
+U16 = mybir.dt.uint16
+U8 = mybir.dt.uint8
+FP8X4 = mybir.dt.float8_e4m3fn_x4
+FP4X4 = mybir.dt.float4_e2m1fn_x4
+ALU = mybir.AluOpType
+ACT = mybir.ActivationFunctionType
+
+P = 128
+PASS = 512
+OPT = dict(gain="SSSSSSVV", conv="VSVSVVVV", add="VVVVVVVV", deal="VVVV", xint="VV", last=2, fin="VV", hold=1, order="0sAB1CD2w4", wide=1)
+
+
+def tile_list_die_link_trunk_kernel(
+    tc, tab_words, tab_scales, offs, pos1, pos2, w1, phase, gain, w2_words, w2_scales,
+    w3, w4_words, w4_scales, base, out_0, out_1, out_2,
+):
+    nc = tc.nc
+    eng = {"V": nc.vector, "S": nc.scalar, "G": nc.gpsimd, "Q": nc.sync}
+    scaled = "G" in OPT["add"]
+    with ExitStack() as ctx:
+        lists = ctx.enter_context(tc.tile_pool(name="lists", bufs=1))
+        keep = ctx.enter_context(tc.tile_pool(name="keep", bufs=1))
+        raws = ctx.enter_context(tc.tile_pool(name="raws", bufs=4))
+        ring = ctx.enter_context(tc.tile_pool(name="ring", bufs=3))
+        pair = ctx.enter_context(tc.tile_pool(name="pair", bufs=2))
+        last = ctx.enter_context(tc.tile_pool(name="last", bufs=1))
+        psum = ctx.enter_context(tc.psum_pool(name="psum", bufs=8))
+
+        def held(shape, dtype, name):
+            return keep.tile(shape, dtype, name=name, align_bytes=64)
+
+        def words_view(dram):
+            return dram.rearrange("p n t -> p (n t)").bitcast(I32)
+
+        offs_t = lists.tile([P, S // 16], U16, name="offs_t")
+        pos1_t = lists.tile([P, P1 // 16], U16, name="pos1_t")
+        pos2_t = lists.tile([P, P2 // 16], U16, name="pos2_t")
+
+        tab_s = held([P, T], U8, "tab_s")
+        ws_raw = held([P, H], U8, "ws_raw")
+        zero = held([P, 1], F32, "zero")
+        nc.vector.memset(tab_s[:].bitcast(I32), 0)
+        nc.vector.memset(ws_raw[:].bitcast(I32), 0)
+        nc.vector.memset(zero[:], 0.0)
+
+        nc.sync.dma_start(offs_t[:], offs)
+        tab_w = [held([P, T], U32, f"tab_w{a}") for a in range(2)]
+        phase_t = held([P, 2, 4], F32, "phase_t")
+        gain_t = held([P, 2, 4], F32, "gain_t")
+        w2_raw = [held([P, H], I32, f"w2_raw{a}") for a in range(2)]
+        w4_raw = held([P, 2 * N], U16, "w4_raw")
+        w1_raw = {}
+
+        def load_rows(w, a, b):
+            raw = raws.tile([P, 4, PASS], F32, name="raw")
+            nc.sync.dma_start(
+                out=raw[:],
+                in_=w[PASS * a : PASS * (a + 1), PASS * b : PASS * (b + 1)].rearrange("(p j) c -> p j c", j=4),
+            )
+            return raw
+
+        for tok in OPT["order"]:
+            if tok in "01":
+                nc.sync.dma_start(out=tab_w[int(tok)][:].bitcast(I32), in_=words_view(tab_words[int(tok)]))
+            if tok == "s":
+                for q in range(4):
+                    nc.sync.dma_start(
+                        out=tab_s[32 * q : 32 * q + 8, :].bitcast(I32),
+                        in_=tab_scales[:, 4 * q : 4 * q + 4, :].bitcast(I32),
+                    )
+            if tok in "ABCD":
+                b, a = divmod("ABCD".index(tok), 2)
+                w1_raw[a, b] = load_rows(w1, a, b)
+            if tok == "B":
+                nc.sync.dma_start(out=phase_t[:], in_=phase.rearrange("(b p t) -> p b t", b=2, t=4))
+                nc.sync.dma_start(pos1_t[:], pos1)
+                nc.sync.dma_start(out=gain_t[:], in_=gain.rearrange("(b p t) -> p b t", b=2, t=4))
+            if tok == "2":
+                nc.sync.dma_start(pos2_t[:], pos2)
+                for a in range(2):
+                    nc.sync.dma_start(out=w2_raw[a][:], in_=words_view(w2_words[a]))
+            if tok == "w":
+                for q in range(4):
+                    nc.sync.dma_start(
+                        out=ws_raw[32 * q + 4 : 32 * q + 12, :].bitcast(I32),
+                        in_=w2_scales[:, 4 * q : 4 * q + 4, :].bitcast(I32),
+                    )
+                    nc.sync.dma_start(
+                        out=ws_raw[32 * q : 32 * q + 4, :].bitcast(I32).rearrange("r (a c) -> r a c", a=2),
+                        in_=w4_scales[:, 4 * q : 4 * q + 4, :].bitcast(I32).rearrange("a r c -> r a c"),
+                    )
+            if tok == "4":
+                nc.sync.dma_start(
+                    out=w4_raw[:].bitcast(I32).rearrange("p (a c) -> p a c", a=2),
+                    in_=w4_words.bitcast(I32).rearrange("a p c -> p a c"),
+                )
+
+        silu0 = held([P, 1], F32, "silu0")
+        half_pi = held([P, 1], F32, "half_pi")
+        nc.scalar.activation(out=silu0[:], in_=zero[:], func=ACT.Silu)
+        nc.vector.tensor_scalar(out=half_pi[:], in0=silu0[:], scalar1=math.pi / 2, scalar2=None, op0=ALU.add)
+        if scaled:
+            gain_in, gain_t = gain_t, held([P, 2, 4], F32, "gain_over")
+            nc.vector.tensor_scalar(out=gain_t[:], in0=gain_in[:], scalar1=1 / 0.9, scalar2=None, op0=ALU.mult)
+
+        v_s = held([P, S], U8, "v_s")
+        nc.vector.tensor_copy(out=v_s[:], in_=tab_s[:].indirect(offs_t[:]))
+        v_w = {}
+        for a in range(2):
+            for h in range(2):
+                v_w[a, h] = held([P, 512], U32, f"v_w{a}{h}")
+                nc.vector.tensor_copy(out=v_w[a, h][:], in_=tab_w[a][:].indirect(offs_t[:, 32 * h : 32 * (h + 1)]))
+
+        def quantise_weight(raw, u, on_scalar, name, tag="grouped"):
+            pool = ring if tag == "grouped" else last
+            grouped = pool.tile([P, 1024], BF16, name="grouped", tag=tag, align_bytes=64)
+            src = raw[:].rearrange("p j (m u e) -> p u m j e", u=2, e=2)[:, u]
+            dst = grouped[:].rearrange("p (e m j) -> p m j e", e=2, j=4)
+            if on_scalar:
+                nc.scalar.copy(out=dst, in_=src)
+            else:
+                nc.vector.tensor_copy(out=dst, in_=src)
+            codes = held([P, 256], U32, name + "_c")
+            scales = held([P, 256], U8, name + "_s")
+            nc.vector.quantize_mx(out=codes[:].bitcast(FP8X4), scales=scales[:], in_=grouped[:])
+            return codes, scales
+
+        def interleave(engine, planes, width, name, factor=None):
+            grouped = pair.tile([P, 4 * width], BF16, name=name, align_bytes=64)
+            dst = grouped[:].rearrange("p (c i t) -> p c t i", i=4, t=4)
+            src = planes.rearrange("p t (c i) -> p c t i", i=4)
+            if engine == "S" and factor is None:
+                nc.scalar.copy(out=dst, in_=src)
+            elif engine == "S":
+                nc.scalar.activation(out=dst, in_=src, func=ACT.Copy, scale=factor)
+            elif factor is None:
+                nc.vector.tensor_copy(out=dst, in_=src)
+            else:
+                nc.vector.tensor_scalar(out=dst, in0=src, scalar1=factor, scalar2=None, op0=ALU.mult)
+            return grouped
+
+        back = 0.9 if scaled else None
+
+        x1 = [held([P, 4, P1], F32, f"x1_{b}") for b in range(2)]
+        x1_c = [held([P, P1], U32, f"x1_c{b}") for b in range(2)]
+        x1_s = [held([P, P1], U8, f"x1_s{b}") for b in range(2)]
+        w1_q = {}
+        for a in range(2):
+            for u in range(2):
+                w1_q[a, 0, u] = quantise_weight(w1_raw[a, 0], u, OPT["conv"][2 * a + u] == "S", f"w1_{a}0{u}")
+
+        def stage1(b, t):
+            u, e = divmod(t, 2)
+            arg = ring.tile([P, S], F32, name="arg")
+            for h in range(2):
+                bank = psum.tile([P, 512], F32, name="bank")
+                for a in range(2):
+                    codes, scales = w1_q[a, b, u]
+                    nc.tensor.matmul_mx(
+                        out=bank[:],
+                        lhsT=codes[:, P * e : P * (e + 1)].bitcast(FP8X4),
+                        lhsT_scale=scales[:, P * e : P * (e + 1)],
+                        rhs=v_w[a, h][:].bitcast(FP8X4),
+                        rhs_scale=v_s[4 * a : P, 512 * h : 512 * (h + 1)],
+                        start=(a == 0), stop=(a == 1),
+                    )
+                nc.scalar.activation(
+                    out=arg[:, 512 * h : 512 * (h + 1)], in_=bank[:], func=ACT.Abs, bias=phase_t[:, b, t : t + 1],
+                )
+            return arg
+
+        def pick1(b, t, arg):
+            final = (b, t) == (1, 3)
+            parts = OPT["last"] if final else 1
+            width = P1 // parts
+            pool = last if final and OPT["hold"] else ring
+            picked = pool.tile([P, P1], F32, name="picked", align_bytes=64)
+            cosine = pool.tile([P, P1], F32, name="cosine", align_bytes=64)
+            for i in range(parts):
+                cols = slice(width * i, width * (i + 1))
+                nc.vector.tensor_copy(out=picked[:, cols], in_=arg[:].indirect(pos1_t[:, width // 16 * i : width // 16 * (i + 1)]))
+            for i in range(parts):
+                cols = slice(width * i, width * (i + 1))
+                nc.scalar.activation(out=cosine[:, cols], in_=picked[:, cols], func=ACT.Sin, bias=half_pi[:], scale=-1.0)
+                who = OPT["gain"][4 * b + t]
+                if who == "S":
+                    nc.scalar.activation(out=x1[b][:, t, cols], in_=cosine[:, cols], func=ACT.Copy, scale=gain_t[:, b, t : t + 1])
+                elif who == "V":
+                    nc.vector.tensor_scalar(out=x1[b][:, t, cols], in0=cosine[:, cols], scalar1=gain_t[:, b, t : t + 1], scalar2=None, op0=ALU.mult)
+                else:
+                    nc.gpsimd.tensor_scalar(out=x1[b][:, t, cols], in0=cosine[:, cols], scalar1=gain_t[:, b, t : t + 1], scalar2=0.0, op0=ALU.mult, op1=ALU.add)
+
+        def quantise_x1(b):
+            parts = OPT["last"] if b == 1 else 1
+            width = P1 // parts
+            groups = []
+            for i in range(parts):
+                cols = slice(width * i, width * (i + 1))
+                groups.append((cols, interleave(OPT["xint"][b], x1[b][:, :, cols], width, "x1_g", back)))
+            for cols, grouped in groups:
+                nc.vector.quantize_mx(out=x1_c[b][:, cols].bitcast(FP8X4), scales=x1_s[b][:, cols], in_=grouped[:])
+
+        w2_w = [held([P, H], I32, f"w2_w{a}") for a in range(2)]
+
+        def deal_w2(a):
+            eng[OPT["deal"][a]].tensor_copy(
+                out=w2_w[a][:].rearrange("p (b t m) -> p b m t", b=2, t=4),
+                in_=w2_raw[a][:].rearrange("p (b m t) -> p b m t", b=2, t=4),
+            )
+
+        slices = [(b, t) for b in range(2) for t in range(4)]
+        args = {}
+        args[0] = stage1(*slices[0])
+        for u in range(2):
+            w1_q[0, 1, u] = quantise_weight(w1_raw[0, 1], u, OPT["conv"][4 + u] == "S", f"w1_01{u}")
+        for s in range(8):
+            if s + 1 < 8:
+                args[s + 1] = stage1(*slices[s + 1])
+            pick1(*slices[s], args[s])
+            if s < 2:
+                w1_q[1, 1, s] = quantise_weight(w1_raw[1, 1], s, OPT["conv"][6 + s] == "S", f"w1_11{s}")
+            if s == 4:
+                quantise_x1(0)
+            if s in (5, 6):
+                deal_w2(s - 5)
+
+        w3_raw = [load_rows(w3, a, 0) for a in range(2)]
+        base_t = held([P, 4, P2], F32, "base_t")
+        nc.sync.dma_start(out=base_t[:], in_=base.rearrange("(p t) j -> p t j", t=4))
+
+        ws = held([P, H], U8, "ws")
+        eng[OPT["deal"][2]].tensor_copy(
+            out=ws[:].rearrange("p (b t m) -> p b m t", b=2, t=4),
+            in_=ws_raw[:].rearrange("p (b m t) -> p b m t", b=2, t=4),
+        )
+
+        w4_w = held([P, 2 * N], U16, "w4_w")
+        nc.vector.tensor_copy(
+            out=w4_w[:].rearrange("p (a t m) -> p a m t", a=2, t=4),
+            in_=w4_raw[:].rearrange("p (a m t) -> p a m t", a=2, t=4),
+        )
+        quantise_x1(1)
+
+        x2 = [held([P, P1], F32, f"x2_{s}") for s in range(8)]
+        x3_low = held([P, 4, P2], F32, "x3_low")
+        x3_high = {0: held([P, 4, P], F32, "x3_high0")}
+        x3_q = {}
+        w3_q = {}
+
+        def stage2(b, t):
+            bank = psum.tile([P, 512], F32, name="bank")
+            cols = slice(PASS * b + P * t, PASS * b + P * (t + 1))
+            for a in range(2):
+                nc.tensor.matmul_mx(
+                    out=bank[:],
+                    lhsT=w2_w[a][:, cols].bitcast(FP8X4),
+                    lhsT_scale=ws[4 + 4 * a : P, cols],
+                    rhs=x1_c[a][:].bitcast(FP8X4),
+                    rhs_scale=x1_s[a][:],
+                    start=(a == 0), stop=(a == 1),
+                )
+            least = ring.tile([P, P1], F32, name="least")
+            if scaled:
+                nc.vector.scalar_tensor_tensor(
+                    out=least[:], in0=x1[b][:, t, :], scalar=0.9, in1=bank[:], op0=ALU.mult, op1=ALU.min,
+                )
+            else:
+                nc.vector.tensor_tensor(out=least[:], in0=bank[:], in1=x1[b][:, t, :], op=ALU.min)
+            return least
+
+        def step(s, least):
+            b, t = slices[s]
+            if scaled:
+                eng[OPT["add"][s]].tensor_tensor(out=x2[s][:], in0=least[:], in1=x1[b][:, t, :], op=ALU.add)
+            else:
+                nc.vector.scalar_tensor_tensor(
+                    out=x2[s][:], in0=least[:], scalar=0.9, in1=x1[b][:, t, :], op0=ALU.mult, op1=ALU.add,
+                )
+
+        def pick2(s, h):
+            b, t = slices[s]
+            if b == 0:
+                nc.vector.tensor_copy(out=x3_low[:, t, :], in_=x2[s][:].indirect(pos2_t[:]))
+            else:
+                nc.vector.tensor_copy(out=x3_high[h][:, t, :], in_=x2[s][:].indirect(pos2_t[:, 8 * h : 8 * (h + 1)]))
+
+        def quantise_x3(b, h):
+            planes = x3_low[:] if b == 0 else x3_high[h][:]
+            width = planes.shape[2]
+            grouped = interleave("S", planes, width, "x3_g", back)
+            codes = held([P, width], U32, f"x3_c{b}{h}")
+            scales = held([P, width], U8, f"x3_s{b}{h}")
+            nc.vector.quantize_mx(out=codes[:].bitcast(FP8X4), scales=scales[:], in_=grouped[:])
+            if b == 0:
+                for i in range(2):
+                    x3_q[0, i] = codes[:, P * i : P * (i + 1)], scales[:, P * i : P * (i + 1)]
+            else:
+                x3_q[1, h] = codes[:], scales[:]
+
+        leasts = {}
+        for s in range(10):
+            if s < 8:
+                leasts[s] = stage2(*slices[s])
+            if 1 <= s < 9:
+                step(s - 1, leasts[s - 1])
+            if s >= 2:
+                pick2(s - 2, 0)
+            if 2 <= s < 6:
+                a, u = divmod(s - 2, 2)
+                w3_q[a, u] = quantise_weight(w3_raw[a], u, True, f"w3_{a}{u}", ("picked", "cosine")[u] if OPT["hold"] else "grouped")
+            if s == 6:
+                quantise_x3(0, 0)
+
+        y_c = held([P, P2], U32, "y_c")
+        y_s = held([P, P2], U8, "y_s")
+        banks3 = {}
+
+        def stage3(a, h):
+            if a == 0:
+                banks3[h] = (psum.tile([P, 4, P], F32, name="bank"), psum.tile([P, 4, P], F32, name="bank"))
+            f_bank, l_bank = banks3[h]
+            codes, scales = x3_q[a, h]
+            for t in range(4):
+                u, e = divmod(t, 2)
+                w_codes, w_scales = w3_q[a, u]
+                nc.tensor.matmul_mx(
+                    out=f_bank[:, t, :],
+                    lhsT=w_codes[:, P * e : P * (e + 1)].bitcast(FP8X4),
+                    lhsT_scale=w_scales[:, P * e : P * (e + 1)],
+                    rhs=codes.bitcast(FP8X4), rhs_scale=scales,
+                    start=(a == 0 and t == 0), stop=(a == 1 and t == 3),
+                )
+            for t in range(4):
+                cols = slice(N * a + P * t, N * a + P * (t + 1))
+                nc.tensor.matmul_mx(
+                    out=l_bank[:, t, :],
+                    lhsT=w4_w[:, cols].bitcast(FP4X4),
+                    lhsT_scale=ws[:, cols],
+                    rhs=codes.bitcast(FP8X4), rhs_scale=scales,
+                    start=(a == 0 and t == 0), stop=(a == 1 and t == 3),
+                )
+
+        def finish(h):
+            f_bank, l_bank = banks3[h]
+            cols = slice(P * h, P * (h + 1))
+            gate = pair.tile([P, 4, P], F32, name="gate")
+            nc.scalar.activation(out=gate[:], in_=f_bank[:], func=ACT.Tanh)
+            link = pair.tile([P, 4, P], F32, name="link")
+            nc.vector.tensor_tensor(out=link[:], in0=l_bank[:], in1=gate[:], op=ALU.mult)
+            y = pair.tile([P, 4, P], F32, name="y")
+            eng[OPT["fin"][h]].tensor_tensor(out=y[:], in0=link[:], in1=base_t[:, :, cols], op=ALU.add)
+            nc.sync.dma_start(out=out_0.rearrange("(p t) j -> p t j", t=4)[:, :, cols], in_=y[:])
+            return y
+
+        def planes(h, y):
+            cols = slice(P * h, P * (h + 1))
+            grouped = interleave("S" if h == 0 else "V", y[:], P, "x3_g")
+            nc.vector.quantize_mx(out=y_c[:, cols].bitcast(FP8X4), scales=y_s[:, cols], in_=grouped[:])
+            nc.sync.dma_start(out=words_view(out_1[0])[:, cols], in_=y_c[:, cols].bitcast(I32))
+
+        stage3(0, 0)
+        stage3(0, 1)
+        x3_high[1] = held([P, 4, P], F32, "x3_high1")
+        for s in range(4, 6):
+            pick2(s, 1)
+        quantise_x3(1, 0)
+        stage3(1, 0)
+        for s in range(6, 8):
+            pick2(s, 1)
+        quantise_x3(1, 1)
+        y0 = finish(0)
+        stage3(1, 1)
+        planes(0, y0)
+        y1 = finish(1)
+        planes(1, y1)
+        for q in range(4):
+            queue = nc.sync if q % 2 == 0 else nc.scalar
+            queue.dma_start(
+                out=out_2[0, 4 * q : 4 * q + 4, :].bitcast(I32),
+                in_=y_s[32 * q : 32 * q + 4, :].bitcast(I32),
+            )

@@ -19,7 +19,7 @@ ACT = mybir.ActivationFunctionType
 
 P = 128
 PASS = 512
-OPT = dict(gain="SSSSSSVV", conv="VSVSVVVV", add="VVVVVVVV", deal="VVVV", xint="VV", last=2, fin="VV", hold=1, order="0sAB1CD2w4", wide=1)
+OPT = dict(gain="SSSSSSVV", conv="SSSSVVVV", add="VVVVVVVV", deal="VVVV", xint="VV", last=2, fin="VV", hold=1, order="ps0AB1CD2w4", move=1, lag=1, skew=2)
 
 
 def tile_list_die_link_trunk_kernel(
@@ -52,11 +52,14 @@ def tile_list_die_link_trunk_kernel(
         ws_raw = held([P, H], U8, "ws_raw")
         zero = held([P, 1], F32, "zero")
         nc.vector.memset(tab_s[:].bitcast(I32), 0)
-        nc.vector.memset(ws_raw[:].bitcast(I32), 0)
+        nc.gpsimd.memset(ws_raw[:].bitcast(I32), 0)
         nc.vector.memset(zero[:], 0.0)
 
+        v_s = [held([P, S], U8, f"v_s{a}") for a in range(2)]
+        for a in range(2 * OPT["move"]):
+            nc.gpsimd.memset(v_s[a][:].bitcast(I32), 0)
         nc.sync.dma_start(offs_t[:], offs)
-        tab_w = [held([P, T], U32, f"tab_w{a}") for a in range(2)]
+        tab_w = [last.tile([P, T], U32, name=f"tab_w{a}", tag=f"wide{a}", align_bytes=64) for a in range(2)]
         phase_t = held([P, 2, 4], F32, "phase_t")
         gain_t = held([P, 2, 4], F32, "gain_t")
         w2_raw = [held([P, H], I32, f"w2_raw{a}") for a in range(2)]
@@ -75,20 +78,26 @@ def tile_list_die_link_trunk_kernel(
             if tok in "01":
                 nc.sync.dma_start(out=tab_w[int(tok)][:].bitcast(I32), in_=words_view(tab_words[int(tok)]))
             if tok == "s":
-                for q in range(4):
+                if OPT["move"]:
                     nc.sync.dma_start(
-                        out=tab_s[32 * q : 32 * q + 8, :].bitcast(I32),
-                        in_=tab_scales[:, 4 * q : 4 * q + 4, :].bitcast(I32),
+                        out=tab_s[0:P:4, :].bitcast(I32),
+                        in_=tab_scales.rearrange("a q n -> (a q) n").bitcast(I32),
                     )
+                else:
+                    for q in range(4):
+                        nc.sync.dma_start(
+                            out=tab_s[32 * q : 32 * q + 8, :].bitcast(I32),
+                            in_=tab_scales[:, 4 * q : 4 * q + 4, :].bitcast(I32),
+                        )
             if tok in "ABCD":
                 b, a = divmod("ABCD".index(tok), 2)
                 w1_raw[a, b] = load_rows(w1, a, b)
-            if tok == "B":
+            if tok == "p":
+                nc.sync.dma_start(pos2_t[:], pos2)
                 nc.sync.dma_start(out=phase_t[:], in_=phase.rearrange("(b p t) -> p b t", b=2, t=4))
                 nc.sync.dma_start(pos1_t[:], pos1)
                 nc.sync.dma_start(out=gain_t[:], in_=gain.rearrange("(b p t) -> p b t", b=2, t=4))
             if tok == "2":
-                nc.sync.dma_start(pos2_t[:], pos2)
                 for a in range(2):
                     nc.sync.dma_start(out=w2_raw[a][:], in_=words_view(w2_words[a]))
             if tok == "w":
@@ -115,8 +124,15 @@ def tile_list_die_link_trunk_kernel(
             gain_in, gain_t = gain_t, held([P, 2, 4], F32, "gain_over")
             nc.vector.tensor_scalar(out=gain_t[:], in0=gain_in[:], scalar1=1 / 0.9, scalar2=None, op0=ALU.mult)
 
-        v_s = held([P, S], U8, "v_s")
-        nc.vector.tensor_copy(out=v_s[:], in_=tab_s[:].indirect(offs_t[:]))
+        spread_s = held([P, S], U8, "spread_s")
+        nc.vector.tensor_copy(out=spread_s[:], in_=tab_s[:].indirect(offs_t[:]))
+        for a in range(2 * OPT["move"]):
+            for q in range(4):
+                first = 4 * (16 * a + 4 * q)
+                nc.gpsimd.dma_start(
+                    out=v_s[a][32 * q : 32 * q + 4, :].bitcast(I32),
+                    in_=spread_s[first : first + 16 : 4, :].bitcast(I32),
+                )
         v_w = {}
         for a in range(2):
             for h in range(2):
@@ -173,7 +189,7 @@ def tile_list_die_link_trunk_kernel(
                         lhsT=codes[:, P * e : P * (e + 1)].bitcast(FP8X4),
                         lhsT_scale=scales[:, P * e : P * (e + 1)],
                         rhs=v_w[a, h][:].bitcast(FP8X4),
-                        rhs_scale=v_s[4 * a : P, 512 * h : 512 * (h + 1)],
+                        rhs_scale=v_s[a][:, 512 * h : 512 * (h + 1)] if OPT["move"] else spread_s[4 * a : P, 512 * h : 512 * (h + 1)],
                         start=(a == 0), stop=(a == 1),
                     )
                 nc.scalar.activation(
@@ -216,8 +232,8 @@ def tile_list_die_link_trunk_kernel(
 
         def deal_w2(a):
             eng[OPT["deal"][a]].tensor_copy(
-                out=w2_w[a][:].rearrange("p (b t m) -> p b m t", b=2, t=4),
-                in_=w2_raw[a][:].rearrange("p (b m t) -> p b m t", b=2, t=4),
+                out=w2_w[a][:].rearrange("p (b t g i) -> p b g t i", b=2, t=4, i=4),
+                in_=w2_raw[a][:].rearrange("p (b g i t) -> p b g t i", b=2, t=4, i=4),
             )
 
         slices = [(b, t) for b in range(2) for t in range(4)]
@@ -242,20 +258,20 @@ def tile_list_die_link_trunk_kernel(
 
         ws = held([P, H], U8, "ws")
         eng[OPT["deal"][2]].tensor_copy(
-            out=ws[:].rearrange("p (b t m) -> p b m t", b=2, t=4),
-            in_=ws_raw[:].rearrange("p (b m t) -> p b m t", b=2, t=4),
+            out=ws[:].rearrange("p (b t m) -> p b t m", b=2, t=4),
+            in_=ws_raw[:].rearrange("p (b m t) -> p b t m", b=2, t=4),
         )
 
         w4_w = held([P, 2 * N], U16, "w4_w")
         nc.vector.tensor_copy(
-            out=w4_w[:].rearrange("p (a t m) -> p a m t", a=2, t=4),
-            in_=w4_raw[:].rearrange("p (a m t) -> p a m t", a=2, t=4),
+            out=w4_w[:].rearrange("p (a t m) -> p a t m", a=2, t=4),
+            in_=w4_raw[:].rearrange("p (a m t) -> p a t m", a=2, t=4),
         )
         quantise_x1(1)
 
         x2 = [held([P, P1], F32, f"x2_{s}") for s in range(8)]
         x3_low = held([P, 4, P2], F32, "x3_low")
-        x3_high = {0: held([P, 4, P], F32, "x3_high0")}
+        x3_high = {0: last.tile([P, 4, P], F32, name="x3_high")}
         x3_q = {}
         w3_q = {}
 
@@ -299,7 +315,7 @@ def tile_list_die_link_trunk_kernel(
         def quantise_x3(b, h):
             planes = x3_low[:] if b == 0 else x3_high[h][:]
             width = planes.shape[2]
-            grouped = interleave("S", planes, width, "x3_g", back)
+            grouped = interleave("V" if b == 1 else "S", planes, width, "x3_g", back)
             codes = held([P, width], U32, f"x3_c{b}{h}")
             scales = held([P, width], U8, f"x3_s{b}{h}")
             nc.vector.quantize_mx(out=codes[:].bitcast(FP8X4), scales=scales[:], in_=grouped[:])
@@ -310,17 +326,17 @@ def tile_list_die_link_trunk_kernel(
                 x3_q[1, h] = codes[:], scales[:]
 
         leasts = {}
-        for s in range(10):
+        for s in range(8 + OPT["skew"]):
             if s < 8:
                 leasts[s] = stage2(*slices[s])
             if 1 <= s < 9:
                 step(s - 1, leasts[s - 1])
-            if s >= 2:
-                pick2(s - 2, 0)
+            if s >= OPT["skew"]:
+                pick2(s - OPT["skew"], 0)
             if 2 <= s < 6:
                 a, u = divmod(s - 2, 2)
-                w3_q[a, u] = quantise_weight(w3_raw[a], u, True, f"w3_{a}{u}", ("picked", "cosine")[u] if OPT["hold"] else "grouped")
-            if s == 6:
+                w3_q[a, u] = quantise_weight(w3_raw[a], u, True, f"w3_{a}{u}", ("picked", "cosine")[u])
+            if s == 3 + OPT["skew"]:
                 quantise_x3(0, 0)
 
         y_c = held([P, P2], U32, "y_c")
@@ -372,12 +388,10 @@ def tile_list_die_link_trunk_kernel(
 
         stage3(0, 0)
         stage3(0, 1)
-        x3_high[1] = held([P, 4, P], F32, "x3_high1")
-        for s in range(4, 6):
-            pick2(s, 1)
         quantise_x3(1, 0)
         stage3(1, 0)
-        for s in range(6, 8):
+        x3_high[1] = last.tile([P, 4, P], F32, name="x3_high")
+        for s in range(4, 8):
             pick2(s, 1)
         quantise_x3(1, 1)
         y0 = finish(0)

@@ -19,7 +19,7 @@ ACT = mybir.ActivationFunctionType
 
 P = 128
 PASS = 512
-OPT = dict(gain="SSSSSSVV", conv="SSSSVVVV", add="VVVVVVVV", deal="VVVV", xint="VV", last=2, fin="VV", hold=1, order="ps0AB1CD2w4", move=1, lag=1, skew=2)
+OPT = dict(gain="SSSSSSVV", conv="SSSSVVVV", add="GGGGGGGV", deal="VVVV", xint="VV", last=2, fin="VV", hold=1, order="ps0AB1CD2w4", move=1, lag=1, skew=2)
 
 
 def tile_list_die_link_trunk_kernel(
@@ -51,7 +51,8 @@ def tile_list_die_link_trunk_kernel(
         tab_s = held([P, T], U8, "tab_s")
         ws_raw = held([P, H], U8, "ws_raw")
         zero = held([P, 1], F32, "zero")
-        nc.vector.memset(tab_s[:].bitcast(I32), 0)
+        nc.vector.memset(tab_s[:, : T // 2].bitcast(I32), 0)
+        nc.gpsimd.memset(tab_s[:, T // 2 :].bitcast(I32), 0)
         nc.gpsimd.memset(ws_raw[:].bitcast(I32), 0)
         nc.vector.memset(zero[:], 0.0)
 
@@ -94,9 +95,9 @@ def tile_list_die_link_trunk_kernel(
                 w1_raw[a, b] = load_rows(w1, a, b)
             if tok == "p":
                 nc.sync.dma_start(pos2_t[:], pos2)
-                nc.sync.dma_start(out=phase_t[:], in_=phase.rearrange("(b p t) -> p b t", b=2, t=4))
                 nc.sync.dma_start(pos1_t[:], pos1)
-                nc.sync.dma_start(out=gain_t[:], in_=gain.rearrange("(b p t) -> p b t", b=2, t=4))
+                nc.scalar.dma_start(out=phase_t[:], in_=phase.rearrange("(b p t) -> p b t", b=2, t=4))
+                nc.scalar.dma_start(out=gain_t[:], in_=gain.rearrange("(b p t) -> p b t", b=2, t=4))
             if tok == "2":
                 for a in range(2):
                     nc.sync.dma_start(out=w2_raw[a][:], in_=words_view(w2_words[a]))

@@ -19,7 +19,15 @@ ACT = mybir.ActivationFunctionType
 
 P = 128
 PASS = 512
-OPT = dict(gain="SSSSSSVV", conv="SSSSVVVV", add="GGGGGGGV", deal="VVVV", xint="VV", last=2, fin="VV", hold=1, order="ps0AB1CD2w4", move=1, lag=1, skew=2)
+BANK = 512
+LIST = 16
+STEP = 0.9
+SLICES = [(b, t) for b in range(2) for t in range(4)]
+
+AHEAD = 2
+GAINS_ON_VECTOR = 2
+SUMS_ON_GPSIMD = 3
+MOVES_ON_GPSIMD = 2
 
 
 def tile_list_die_link_trunk_kernel(
@@ -27,328 +35,294 @@ def tile_list_die_link_trunk_kernel(
     w3, w4_words, w4_scales, base, out_0, out_1, out_2,
 ):
     nc = tc.nc
-    eng = {"V": nc.vector, "S": nc.scalar, "G": nc.gpsimd, "Q": nc.sync}
-    scaled = "G" in OPT["add"]
     with ExitStack() as ctx:
         lists = ctx.enter_context(tc.tile_pool(name="lists", bufs=1))
         keep = ctx.enter_context(tc.tile_pool(name="keep", bufs=1))
-        raws = ctx.enter_context(tc.tile_pool(name="raws", bufs=4))
+        raws = ctx.enter_context(tc.tile_pool(name="raws", bufs=2))
         ring = ctx.enter_context(tc.tile_pool(name="ring", bufs=3))
         pair = ctx.enter_context(tc.tile_pool(name="pair", bufs=2))
-        last = ctx.enter_context(tc.tile_pool(name="last", bufs=1))
+        chain = ctx.enter_context(tc.tile_pool(name="chain", bufs=1))
         psum = ctx.enter_context(tc.psum_pool(name="psum", bufs=8))
 
         def held(shape, dtype, name):
             return keep.tile(shape, dtype, name=name, align_bytes=64)
 
-        def words_view(dram):
-            return dram.rearrange("p n t -> p (n t)").bitcast(I32)
+        def as_words(dram):
+            return dram.rearrange("p n i -> p (n i)").bitcast(I32)
 
-        offs_t = lists.tile([P, S // 16], U16, name="offs_t")
-        pos1_t = lists.tile([P, P1 // 16], U16, name="pos1_t")
-        pos2_t = lists.tile([P, P2 // 16], U16, name="pos2_t")
-
-        tab_s = held([P, T], U8, "tab_s")
-        ws_raw = held([P, H], U8, "ws_raw")
-        zero = held([P, 1], F32, "zero")
-        nc.vector.memset(tab_s[:, : T // 2].bitcast(I32), 0)
-        nc.gpsimd.memset(tab_s[:, T // 2 :].bitcast(I32), 0)
-        nc.gpsimd.memset(ws_raw[:].bitcast(I32), 0)
-        nc.vector.memset(zero[:], 0.0)
-
-        v_s = [held([P, S], U8, f"v_s{a}") for a in range(2)]
-        for a in range(2 * OPT["move"]):
-            nc.gpsimd.memset(v_s[a][:].bitcast(I32), 0)
-        nc.sync.dma_start(offs_t[:], offs)
-        tab_w = [last.tile([P, T], U32, name=f"tab_w{a}", tag=f"wide{a}", align_bytes=64) for a in range(2)]
-        phase_t = held([P, 2, 4], F32, "phase_t")
-        gain_t = held([P, 2, 4], F32, "gain_t")
-        w2_raw = [held([P, H], I32, f"w2_raw{a}") for a in range(2)]
-        w4_raw = held([P, 2 * N], U16, "w4_raw")
-        w1_raw = {}
-
-        def load_rows(w, a, b):
+        def load_block(w, a, b):
             raw = raws.tile([P, 4, PASS], F32, name="raw")
-            nc.sync.dma_start(
-                out=raw[:],
-                in_=w[PASS * a : PASS * (a + 1), PASS * b : PASS * (b + 1)].rearrange("(p j) c -> p j c", j=4),
-            )
+            rows = w[PASS * a : PASS * (a + 1), PASS * b : PASS * (b + 1)]
+            nc.sync.dma_start(out=raw[:], in_=rows.rearrange("(p i) c -> p i c", i=4))
             return raw
 
-        for tok in OPT["order"]:
-            if tok in "01":
-                nc.sync.dma_start(out=tab_w[int(tok)][:].bitcast(I32), in_=words_view(tab_words[int(tok)]))
-            if tok == "s":
-                if OPT["move"]:
-                    nc.sync.dma_start(
-                        out=tab_s[0:P:4, :].bitcast(I32),
-                        in_=tab_scales.rearrange("a q n -> (a q) n").bitcast(I32),
-                    )
-                else:
-                    for q in range(4):
-                        nc.sync.dma_start(
-                            out=tab_s[32 * q : 32 * q + 8, :].bitcast(I32),
-                            in_=tab_scales[:, 4 * q : 4 * q + 4, :].bitcast(I32),
-                        )
-            if tok in "ABCD":
-                b, a = divmod("ABCD".index(tok), 2)
-                w1_raw[a, b] = load_rows(w1, a, b)
-            if tok == "p":
-                nc.sync.dma_start(pos2_t[:], pos2)
-                nc.sync.dma_start(pos1_t[:], pos1)
-                nc.scalar.dma_start(out=phase_t[:], in_=phase.rearrange("(b p t) -> p b t", b=2, t=4))
-                nc.scalar.dma_start(out=gain_t[:], in_=gain.rearrange("(b p t) -> p b t", b=2, t=4))
-            if tok == "2":
-                for a in range(2):
-                    nc.sync.dma_start(out=w2_raw[a][:], in_=words_view(w2_words[a]))
-            if tok == "w":
-                for q in range(4):
-                    nc.sync.dma_start(
-                        out=ws_raw[32 * q + 4 : 32 * q + 12, :].bitcast(I32),
-                        in_=w2_scales[:, 4 * q : 4 * q + 4, :].bitcast(I32),
-                    )
-                    nc.sync.dma_start(
-                        out=ws_raw[32 * q : 32 * q + 4, :].bitcast(I32).rearrange("r (a c) -> r a c", a=2),
-                        in_=w4_scales[:, 4 * q : 4 * q + 4, :].bitcast(I32).rearrange("a r c -> r a c"),
-                    )
-            if tok == "4":
-                nc.sync.dma_start(
-                    out=w4_raw[:].bitcast(I32).rearrange("p (a c) -> p a c", a=2),
-                    in_=w4_words.bitcast(I32).rearrange("a p c -> p a c"),
-                )
-
-        silu0 = held([P, 1], F32, "silu0")
-        half_pi = held([P, 1], F32, "half_pi")
-        nc.scalar.activation(out=silu0[:], in_=zero[:], func=ACT.Silu)
-        nc.vector.tensor_scalar(out=half_pi[:], in0=silu0[:], scalar1=math.pi / 2, scalar2=None, op0=ALU.add)
-        if scaled:
-            gain_in, gain_t = gain_t, held([P, 2, 4], F32, "gain_over")
-            nc.vector.tensor_scalar(out=gain_t[:], in0=gain_in[:], scalar1=1 / 0.9, scalar2=None, op0=ALU.mult)
-
-        spread_s = held([P, S], U8, "spread_s")
-        nc.vector.tensor_copy(out=spread_s[:], in_=tab_s[:].indirect(offs_t[:]))
-        for a in range(2 * OPT["move"]):
-            for q in range(4):
-                first = 4 * (16 * a + 4 * q)
-                nc.gpsimd.dma_start(
-                    out=v_s[a][32 * q : 32 * q + 4, :].bitcast(I32),
-                    in_=spread_s[first : first + 16 : 4, :].bitcast(I32),
-                )
-        v_w = {}
-        for a in range(2):
-            for h in range(2):
-                v_w[a, h] = held([P, 512], U32, f"v_w{a}{h}")
-                nc.vector.tensor_copy(out=v_w[a, h][:], in_=tab_w[a][:].indirect(offs_t[:, 32 * h : 32 * (h + 1)]))
-
-        def quantise_weight(raw, u, on_scalar, name, tag="grouped"):
-            pool = ring if tag == "grouped" else last
-            grouped = pool.tile([P, 1024], BF16, name="grouped", tag=tag, align_bytes=64)
-            src = raw[:].rearrange("p j (m u e) -> p u m j e", u=2, e=2)[:, u]
-            dst = grouped[:].rearrange("p (e m j) -> p m j e", e=2, j=4)
+        def quantise_weight(raw, u, on_scalar, grouped, name):
+            src = raw[:].rearrange("p i (m u e) -> p u m i e", u=2, e=2)[:, u]
+            dst = grouped[:].rearrange("p (e m i) -> p m i e", e=2, i=4)
             if on_scalar:
                 nc.scalar.copy(out=dst, in_=src)
             else:
                 nc.vector.tensor_copy(out=dst, in_=src)
-            codes = held([P, 256], U32, name + "_c")
-            scales = held([P, 256], U8, name + "_s")
+            codes = held([P, 2 * P], U32, name + "_codes")
+            scales = held([P, 2 * P], U8, name + "_scales")
             nc.vector.quantize_mx(out=codes[:].bitcast(FP8X4), scales=scales[:], in_=grouped[:])
             return codes, scales
 
-        def interleave(engine, planes, width, name, factor=None):
-            grouped = pair.tile([P, 4 * width], BF16, name=name, align_bytes=64)
-            dst = grouped[:].rearrange("p (c i t) -> p c t i", i=4, t=4)
-            src = planes.rearrange("p t (c i) -> p c t i", i=4)
-            if engine == "S" and factor is None:
-                nc.scalar.copy(out=dst, in_=src)
-            elif engine == "S":
-                nc.scalar.activation(out=dst, in_=src, func=ACT.Copy, scale=factor)
-            elif factor is None:
-                nc.vector.tensor_copy(out=dst, in_=src)
-            else:
-                nc.vector.tensor_scalar(out=dst, in0=src, scalar1=factor, scalar2=None, op0=ALU.mult)
-            return grouped
+        def side_by_side(slices, name):
+            grouped = pair.tile([P, 4 * slices.shape[2]], BF16, name=name, align_bytes=64)
+            dst = grouped[:].rearrange("p (c n t) -> p c t n", n=4, t=4)
+            src = slices.rearrange("p t (c n) -> p c t n", n=4)
+            return grouped, dst, src
 
-        back = 0.9 if scaled else None
+        offs_t = lists.tile([P, S // LIST], U16, name="offs_t")
+        pos1_t = lists.tile([P, P1 // LIST], U16, name="pos1_t")
+        pos2_t = lists.tile([P, P2 // LIST], U16, name="pos2_t")
 
-        x1 = [held([P, 4, P1], F32, f"x1_{b}") for b in range(2)]
-        x1_c = [held([P, P1], U32, f"x1_c{b}") for b in range(2)]
-        x1_s = [held([P, P1], U8, f"x1_s{b}") for b in range(2)]
-        w1_q = {}
+        tab_s = held([P, T], U8, "tab_s")
+        zero = held([P, 1], F32, "zero")
+        nc.vector.memset(tab_s[:, : T // 2].bitcast(I32), 0)
+        nc.gpsimd.memset(tab_s[:, T // 2 :].bitcast(I32), 0)
+        nc.vector.memset(zero[:], 0.0)
+        v_s = [held([P, S], U8, f"v_s{a}") for a in range(2)]
         for a in range(2):
-            for u in range(2):
-                w1_q[a, 0, u] = quantise_weight(w1_raw[a, 0], u, OPT["conv"][2 * a + u] == "S", f"w1_{a}0{u}")
+            nc.gpsimd.memset(v_s[a][:].bitcast(I32), 0)
 
-        def stage1(b, t):
+        tab_w = [chain.tile([P, T], U32, name=f"tab_w{a}", tag=f"wide{a}", align_bytes=64) for a in range(2)]
+        phase_t = held([P, 2, 4], F32, "phase_t")
+        gain_t = held([P, 2, 4], F32, "gain_t")
+        nc.sync.dma_start(offs_t[:], offs)
+        nc.sync.dma_start(pos2_t[:], pos2)
+        nc.sync.dma_start(pos1_t[:], pos1)
+        nc.scalar.dma_start(out=phase_t[:], in_=phase.rearrange("(b p t) -> p b t", b=2, t=4))
+        nc.scalar.dma_start(out=gain_t[:], in_=gain.rearrange("(b p t) -> p b t", b=2, t=4))
+        nc.sync.dma_start(
+            out=tab_s[0:P:4, :].bitcast(I32),
+            in_=tab_scales.rearrange("a q n -> (a q) n").bitcast(I32),
+        )
+        w1_raw = {}
+        for a in range(2):
+            nc.sync.dma_start(out=tab_w[a][:].bitcast(I32), in_=as_words(tab_words[a]))
+            w1_raw[a, 0] = load_block(w1, a, 0)
+        for a in range(2):
+            w1_raw[a, 1] = load_block(w1, a, 1)
+        w2_raw = raws.tile([P, 2, H], I32, name="w2_raw", tag="raw")
+        nc.sync.dma_start(out=w2_raw[:], in_=w2_words.rearrange("a p n i -> p a (n i)").bitcast(I32))
+
+        silu_zero = held([P, 1], F32, "silu_zero")
+        half_pi = held([P, 1], F32, "half_pi")
+        nc.scalar.activation(out=silu_zero[:], in_=zero[:], func=ACT.Silu)
+        nc.vector.tensor_scalar(out=half_pi[:], in0=silu_zero[:], scalar1=math.pi / 2, scalar2=None, op0=ALU.add)
+        z_gain = held([P, 2, 4], F32, "z_gain")
+        nc.vector.tensor_scalar(out=z_gain[:], in0=gain_t[:], scalar1=1 / STEP, scalar2=None, op0=ALU.mult)
+
+        spread_s = held([P, S], U8, "spread_s")
+        nc.vector.tensor_copy(out=spread_s[:], in_=tab_s[:].indirect(offs_t[:]))
+        for a in range(2):
+            for g in range(4):
+                first = 4 * (16 * a + 4 * g)
+                queue = nc.gpsimd if 4 * a + g < MOVES_ON_GPSIMD else nc.scalar
+                queue.dma_start(
+                    out=v_s[a][32 * g : 32 * g + 4, :].bitcast(I32),
+                    in_=spread_s[first : first + 16 : 4, :].bitcast(I32),
+                )
+        v_w = {}
+        for a in range(2):
+            for c in range(S // BANK):
+                v_w[a, c] = held([P, BANK], U32, f"v_w{a}{c}")
+                entries = offs_t[:, BANK // LIST * c : BANK // LIST * (c + 1)]
+                nc.vector.tensor_copy(out=v_w[a, c][:], in_=tab_w[a][:].indirect(entries))
+
+        ws_raw = chain.tile([P, H], U8, name="ws_raw", tag="wide1", align_bytes=64)
+        nc.gpsimd.memset(ws_raw[:].bitcast(I32), 0)
+        for g in range(4):
+            nc.sync.dma_start(
+                out=ws_raw[32 * g + 4 : 32 * g + 12, :].bitcast(I32),
+                in_=w2_scales[:, 4 * g : 4 * g + 4, :].bitcast(I32),
+            )
+            nc.sync.dma_start(
+                out=ws_raw[32 * g : 32 * g + 4, :].bitcast(I32).rearrange("r (a c) -> r a c", a=2),
+                in_=w4_scales[:, 4 * g : 4 * g + 4, :].bitcast(I32).rearrange("a r c -> r a c"),
+            )
+
+        z = [held([P, 4, P1], F32, f"z{b}") for b in range(2)]
+        x1_codes = [held([P, P1], U32, f"x1_codes{b}") for b in range(2)]
+        x1_scales = [held([P, P1], U8, f"x1_scales{b}") for b in range(2)]
+        w1_q = {}
+
+        def quantise_w1(a, b, u):
+            on_scalar = u == 1 if a == 1 else b == 0
+            grouped = ring.tile([P, 2 * PASS], BF16, name="grouped", align_bytes=64)
+            w1_q[a, b, u] = quantise_weight(w1_raw[a, b], u, on_scalar, grouped, f"w1_{a}{b}{u}")
+
+        def first_product(b, t):
             u, e = divmod(t, 2)
-            arg = ring.tile([P, S], F32, name="arg")
-            for h in range(2):
-                bank = psum.tile([P, 512], F32, name="bank")
+            angle = ring.tile([P, S], F32, name="angle", bufs=AHEAD + 2)
+            for c in range(S // BANK):
+                cols = slice(BANK * c, BANK * (c + 1))
+                bank = psum.tile([P, BANK], F32, name="bank")
                 for a in range(2):
                     codes, scales = w1_q[a, b, u]
                     nc.tensor.matmul_mx(
                         out=bank[:],
                         lhsT=codes[:, P * e : P * (e + 1)].bitcast(FP8X4),
                         lhsT_scale=scales[:, P * e : P * (e + 1)],
-                        rhs=v_w[a, h][:].bitcast(FP8X4),
-                        rhs_scale=v_s[a][:, 512 * h : 512 * (h + 1)] if OPT["move"] else spread_s[4 * a : P, 512 * h : 512 * (h + 1)],
-                        start=(a == 0), stop=(a == 1),
+                        rhs=v_w[a, c][:].bitcast(FP8X4),
+                        rhs_scale=v_s[a][:, cols],
+                        start=(a == 0),
+                        stop=(a == 1),
                     )
-                nc.scalar.activation(
-                    out=arg[:, 512 * h : 512 * (h + 1)], in_=bank[:], func=ACT.Abs, bias=phase_t[:, b, t : t + 1],
-                )
-            return arg
+                nc.scalar.activation(out=angle[:, cols], in_=bank[:], func=ACT.Abs, bias=phase_t[:, b, t : t + 1])
+            return angle
 
-        def pick1(b, t, arg):
-            final = (b, t) == (1, 3)
-            parts = OPT["last"] if final else 1
-            width = P1 // parts
-            pool = last if final and OPT["hold"] else ring
+        def pick_by_pos1(s, angle):
+            b, t = SLICES[s]
+            is_last = s == len(SLICES) - 1
+            width = P1 // 2 if is_last else P1
+            pool = chain if is_last else ring
             picked = pool.tile([P, P1], F32, name="picked", align_bytes=64)
             cosine = pool.tile([P, P1], F32, name="cosine", align_bytes=64)
-            for i in range(parts):
-                cols = slice(width * i, width * (i + 1))
-                nc.vector.tensor_copy(out=picked[:, cols], in_=arg[:].indirect(pos1_t[:, width // 16 * i : width // 16 * (i + 1)]))
-            for i in range(parts):
-                cols = slice(width * i, width * (i + 1))
-                nc.scalar.activation(out=cosine[:, cols], in_=picked[:, cols], func=ACT.Sin, bias=half_pi[:], scale=-1.0)
-                who = OPT["gain"][4 * b + t]
-                if who == "S":
-                    nc.scalar.activation(out=x1[b][:, t, cols], in_=cosine[:, cols], func=ACT.Copy, scale=gain_t[:, b, t : t + 1])
-                elif who == "V":
-                    nc.vector.tensor_scalar(out=x1[b][:, t, cols], in0=cosine[:, cols], scalar1=gain_t[:, b, t : t + 1], scalar2=None, op0=ALU.mult)
+            for c0 in range(0, P1, width):
+                entries = pos1_t[:, c0 // LIST : (c0 + width) // LIST]
+                nc.vector.tensor_copy(out=picked[:, c0 : c0 + width], in_=angle[:].indirect(entries))
+            for c0 in range(0, P1, width):
+                cols = slice(c0, c0 + width)
+                nc.scalar.activation(
+                    out=cosine[:, cols], in_=picked[:, cols], func=ACT.Sin, bias=half_pi[:], scale=-1.0,
+                )
+                factor = z_gain[:, b, t : t + 1]
+                if s < len(SLICES) - GAINS_ON_VECTOR:
+                    nc.scalar.activation(out=z[b][:, t, cols], in_=cosine[:, cols], func=ACT.Copy, scale=factor)
                 else:
-                    nc.gpsimd.tensor_scalar(out=x1[b][:, t, cols], in0=cosine[:, cols], scalar1=gain_t[:, b, t : t + 1], scalar2=0.0, op0=ALU.mult, op1=ALU.add)
+                    nc.vector.tensor_scalar(
+                        out=z[b][:, t, cols], in0=cosine[:, cols], scalar1=factor, scalar2=None, op0=ALU.mult,
+                    )
 
-        def quantise_x1(b):
-            parts = OPT["last"] if b == 1 else 1
-            width = P1 // parts
+        def quantise_x1(b, width):
             groups = []
-            for i in range(parts):
-                cols = slice(width * i, width * (i + 1))
-                groups.append((cols, interleave(OPT["xint"][b], x1[b][:, :, cols], width, "x1_g", back)))
+            for c0 in range(0, P1, width):
+                cols = slice(c0, c0 + width)
+                grouped, dst, src = side_by_side(z[b][:, :, cols], "x1_grouped")
+                nc.vector.tensor_scalar(out=dst, in0=src, scalar1=STEP, scalar2=None, op0=ALU.mult)
+                groups.append((cols, grouped))
             for cols, grouped in groups:
-                nc.vector.quantize_mx(out=x1_c[b][:, cols].bitcast(FP8X4), scales=x1_s[b][:, cols], in_=grouped[:])
+                nc.vector.quantize_mx(
+                    out=x1_codes[b][:, cols].bitcast(FP8X4), scales=x1_scales[b][:, cols], in_=grouped[:],
+                )
 
         w2_w = [held([P, H], I32, f"w2_w{a}") for a in range(2)]
 
         def deal_w2(a):
-            eng[OPT["deal"][a]].tensor_copy(
-                out=w2_w[a][:].rearrange("p (b t g i) -> p b g t i", b=2, t=4, i=4),
-                in_=w2_raw[a][:].rearrange("p (b g i t) -> p b g t i", b=2, t=4, i=4),
+            nc.vector.tensor_copy(
+                out=w2_w[a][:].rearrange("p (b t g n) -> p b g t n", b=2, t=4, n=4),
+                in_=w2_raw[:, a, :].rearrange("p (b g n t) -> p b g t n", b=2, t=4, n=4),
             )
 
-        slices = [(b, t) for b in range(2) for t in range(4)]
-        args = {}
-        args[0] = stage1(*slices[0])
+        for a in range(2):
+            for u in range(2):
+                quantise_w1(a, 0, u)
+        angles = {s: first_product(*SLICES[s]) for s in range(AHEAD)}
         for u in range(2):
-            w1_q[0, 1, u] = quantise_weight(w1_raw[0, 1], u, OPT["conv"][4 + u] == "S", f"w1_01{u}")
-        for s in range(8):
-            if s + 1 < 8:
-                args[s + 1] = stage1(*slices[s + 1])
-            pick1(*slices[s], args[s])
+            quantise_w1(0, 1, u)
+        for s in range(len(SLICES)):
             if s < 2:
-                w1_q[1, 1, s] = quantise_weight(w1_raw[1, 1], s, OPT["conv"][6 + s] == "S", f"w1_11{s}")
-            if s == 4:
-                quantise_x1(0)
-            if s in (5, 6):
-                deal_w2(s - 5)
+                quantise_w1(1, 1, s)
+            if s + AHEAD < len(SLICES):
+                angles[s + AHEAD] = first_product(*SLICES[s + AHEAD])
+            pick_by_pos1(s, angles[s])
+            if SLICES[s] == (1, 0):
+                quantise_x1(0, P1)
+            if SLICES[s] in ((1, 1), (1, 2)):
+                deal_w2(SLICES[s][1] - 1)
 
-        w3_raw = [load_rows(w3, a, 0) for a in range(2)]
-        base_t = held([P, 4, P2], F32, "base_t")
-        nc.sync.dma_start(out=base_t[:], in_=base.rearrange("(p t) j -> p t j", t=4))
-
+        w3_raw = [load_block(w3, a, 0) for a in range(2)]
         ws = held([P, H], U8, "ws")
-        eng[OPT["deal"][2]].tensor_copy(
+        nc.vector.tensor_copy(
             out=ws[:].rearrange("p (b t m) -> p b t m", b=2, t=4),
             in_=ws_raw[:].rearrange("p (b m t) -> p b t m", b=2, t=4),
         )
-
+        w4_raw = chain.tile([P, 2 * N], U16, name="w4_raw", tag="wide1", align_bytes=64)
+        nc.sync.dma_start(
+            out=w4_raw[:].bitcast(I32).rearrange("p (a c) -> p a c", a=2),
+            in_=w4_words.bitcast(I32).rearrange("a p c -> p a c"),
+        )
         w4_w = held([P, 2 * N], U16, "w4_w")
         nc.vector.tensor_copy(
             out=w4_w[:].rearrange("p (a t m) -> p a t m", a=2, t=4),
             in_=w4_raw[:].rearrange("p (a m t) -> p a t m", a=2, t=4),
         )
-        quantise_x1(1)
+        base_t = chain.tile([P, 4, P2], F32, name="base_t", tag="wide1", align_bytes=64)
+        nc.sync.dma_start(out=base_t[:], in_=base.rearrange("(p t) j -> p t j", t=4))
+        quantise_x1(1, P1 // 2)
 
-        x2 = [held([P, P1], F32, f"x2_{s}") for s in range(8)]
-        x3_low = held([P, 4, P2], F32, "x3_low")
-        x3_high = {0: last.tile([P, 4, P], F32, name="x3_high")}
-        x3_q = {}
-        w3_q = {}
+        stepped = [held([P, P1], F32, f"stepped{s}") for s in range(len(SLICES))]
 
-        def stage2(b, t):
-            bank = psum.tile([P, 512], F32, name="bank")
+        def least_of(b, t):
+            bank = psum.tile([P, BANK], F32, name="bank")
             cols = slice(PASS * b + P * t, PASS * b + P * (t + 1))
             for a in range(2):
                 nc.tensor.matmul_mx(
                     out=bank[:],
                     lhsT=w2_w[a][:, cols].bitcast(FP8X4),
                     lhsT_scale=ws[4 + 4 * a : P, cols],
-                    rhs=x1_c[a][:].bitcast(FP8X4),
-                    rhs_scale=x1_s[a][:],
-                    start=(a == 0), stop=(a == 1),
+                    rhs=x1_codes[a][:].bitcast(FP8X4),
+                    rhs_scale=x1_scales[a][:],
+                    start=(a == 0),
+                    stop=(a == 1),
                 )
-            least = ring.tile([P, P1], F32, name="least")
-            if scaled:
-                nc.vector.scalar_tensor_tensor(
-                    out=least[:], in0=x1[b][:, t, :], scalar=0.9, in1=bank[:], op0=ALU.mult, op1=ALU.min,
-                )
-            else:
-                nc.vector.tensor_tensor(out=least[:], in0=bank[:], in1=x1[b][:, t, :], op=ALU.min)
+            least = held([P, P1], F32, f"least{b}{t}")
+            nc.vector.scalar_tensor_tensor(
+                out=least[:], in0=z[b][:, t, :], scalar=STEP, in1=bank[:], op0=ALU.mult, op1=ALU.min,
+            )
             return least
 
-        def step(s, least):
-            b, t = slices[s]
-            if scaled:
-                eng[OPT["add"][s]].tensor_tensor(out=x2[s][:], in0=least[:], in1=x1[b][:, t, :], op=ALU.add)
-            else:
-                nc.vector.scalar_tensor_tensor(
-                    out=x2[s][:], in0=least[:], scalar=0.9, in1=x1[b][:, t, :], op0=ALU.mult, op1=ALU.add,
-                )
+        def step(engine, s):
+            b, t = SLICES[s]
+            engine.tensor_tensor(out=stepped[s][:], in0=leasts[s][:], in1=z[b][:, t, :], op=ALU.add)
 
-        def pick2(s, h):
-            b, t = slices[s]
-            if b == 0:
-                nc.vector.tensor_copy(out=x3_low[:, t, :], in_=x2[s][:].indirect(pos2_t[:]))
-            else:
-                nc.vector.tensor_copy(out=x3_high[h][:, t, :], in_=x2[s][:].indirect(pos2_t[:, 8 * h : 8 * (h + 1)]))
+        def pick_by_pos2(b, picks, c0):
+            width = picks[:].shape[2]
+            entries = pos2_t[:, c0 // LIST : (c0 + width) // LIST]
+            for t in range(4):
+                nc.vector.tensor_copy(out=picks[:, t, :], in_=stepped[4 * b + t][:].indirect(entries))
 
-        def quantise_x3(b, h):
-            planes = x3_low[:] if b == 0 else x3_high[h][:]
-            width = planes.shape[2]
-            grouped = interleave("V" if b == 1 else "S", planes, width, "x3_g", back)
-            codes = held([P, width], U32, f"x3_c{b}{h}")
-            scales = held([P, width], U8, f"x3_s{b}{h}")
+        def quantise_x3(picks, on_scalar, name):
+            width = picks[:].shape[2]
+            grouped, dst, src = side_by_side(picks[:], "x3_grouped")
+            if on_scalar:
+                nc.scalar.activation(out=dst, in_=src, func=ACT.Copy, scale=STEP)
+            else:
+                nc.vector.tensor_scalar(out=dst, in0=src, scalar1=STEP, scalar2=None, op0=ALU.mult)
+            codes = held([P, width], U32, name + "_codes")
+            scales = held([P, width], U8, name + "_scales")
             nc.vector.quantize_mx(out=codes[:].bitcast(FP8X4), scales=scales[:], in_=grouped[:])
-            if b == 0:
-                for i in range(2):
-                    x3_q[0, i] = codes[:, P * i : P * (i + 1)], scales[:, P * i : P * (i + 1)]
-            else:
-                x3_q[1, h] = codes[:], scales[:]
+            return codes, scales
 
-        leasts = {}
-        for s in range(8 + OPT["skew"]):
-            if s < 8:
-                leasts[s] = stage2(*slices[s])
-            if 1 <= s < 9:
-                step(s - 1, leasts[s - 1])
-            if s >= OPT["skew"]:
-                pick2(s - OPT["skew"], 0)
-            if 2 <= s < 6:
-                a, u = divmod(s - 2, 2)
-                w3_q[a, u] = quantise_weight(w3_raw[a], u, True, f"w3_{a}{u}", ("picked", "cosine")[u])
-            if s == 3 + OPT["skew"]:
-                quantise_x3(0, 0)
+        leasts = [least_of(b, t) for b, t in SLICES]
+        for s in range(SUMS_ON_GPSIMD):
+            step(nc.gpsimd, s)
+        w3_q = {}
+        for a in range(2):
+            for u in range(2):
+                grouped = chain.tile(
+                    [P, 2 * PASS], BF16, name="w3_grouped", tag=("picked", "cosine")[u], align_bytes=64,
+                )
+                w3_q[a, u] = quantise_weight(w3_raw[a], u, True, grouped, f"w3_{a}{u}")
 
-        y_c = held([P, P2], U32, "y_c")
-        y_s = held([P, P2], U8, "y_s")
-        banks3 = {}
+        for s in range(SUMS_ON_GPSIMD, 4):
+            step(nc.vector, s)
+        picks_low = held([P, 4, P2], F32, "picks_low")
+        pick_by_pos2(0, picks_low, 0)
+        for s in range(4, 6):
+            step(nc.vector, s)
+        x3_low = quantise_x3(picks_low, True, "x3_low")
+        for s in range(6, 8):
+            step(nc.vector, s)
 
-        def stage3(a, h):
-            if a == 0:
-                banks3[h] = (psum.tile([P, 4, P], F32, name="bank"), psum.tile([P, 4, P], F32, name="bank"))
-            f_bank, l_bank = banks3[h]
-            codes, scales = x3_q[a, h]
+        y_codes = held([P, P2], U32, "y_codes")
+        y_scales = held([P, P2], U8, "y_scales")
+
+        def last_products(a, banks, codes, scales):
+            f_bank, l_bank = banks
             for t in range(4):
                 u, e = divmod(t, 2)
                 w_codes, w_scales = w3_q[a, u]
@@ -356,8 +330,10 @@ def tile_list_die_link_trunk_kernel(
                     out=f_bank[:, t, :],
                     lhsT=w_codes[:, P * e : P * (e + 1)].bitcast(FP8X4),
                     lhsT_scale=w_scales[:, P * e : P * (e + 1)],
-                    rhs=codes.bitcast(FP8X4), rhs_scale=scales,
-                    start=(a == 0 and t == 0), stop=(a == 1 and t == 3),
+                    rhs=codes.bitcast(FP8X4),
+                    rhs_scale=scales,
+                    start=(a == 0 and t == 0),
+                    stop=(a == 1 and t == 3),
                 )
             for t in range(4):
                 cols = slice(N * a + P * t, N * a + P * (t + 1))
@@ -365,44 +341,55 @@ def tile_list_die_link_trunk_kernel(
                     out=l_bank[:, t, :],
                     lhsT=w4_w[:, cols].bitcast(FP4X4),
                     lhsT_scale=ws[:, cols],
-                    rhs=codes.bitcast(FP8X4), rhs_scale=scales,
-                    start=(a == 0 and t == 0), stop=(a == 1 and t == 3),
+                    rhs=codes.bitcast(FP8X4),
+                    rhs_scale=scales,
+                    start=(a == 0 and t == 0),
+                    stop=(a == 1 and t == 3),
                 )
 
-        def finish(h):
-            f_bank, l_bank = banks3[h]
-            cols = slice(P * h, P * (h + 1))
+        def pick_high(half):
+            picks_high = chain.tile([P, 4, P], F32, name="picks_high")
+            pick_by_pos2(1, picks_high, P * half)
+            return picks_high
+
+        def link_index(half):
+            f_bank, l_bank = half_banks[half]
+            cols = slice(P * half, P * (half + 1))
             gate = pair.tile([P, 4, P], F32, name="gate")
             nc.scalar.activation(out=gate[:], in_=f_bank[:], func=ACT.Tanh)
             link = pair.tile([P, 4, P], F32, name="link")
             nc.vector.tensor_tensor(out=link[:], in0=l_bank[:], in1=gate[:], op=ALU.mult)
             y = pair.tile([P, 4, P], F32, name="y")
-            eng[OPT["fin"][h]].tensor_tensor(out=y[:], in0=link[:], in1=base_t[:, :, cols], op=ALU.add)
+            nc.vector.tensor_tensor(out=y[:], in0=link[:], in1=base_t[:, :, cols], op=ALU.add)
             nc.sync.dma_start(out=out_0.rearrange("(p t) j -> p t j", t=4)[:, :, cols], in_=y[:])
             return y
 
-        def planes(h, y):
-            cols = slice(P * h, P * (h + 1))
-            grouped = interleave("S" if h == 0 else "V", y[:], P, "x3_g")
-            nc.vector.quantize_mx(out=y_c[:, cols].bitcast(FP8X4), scales=y_s[:, cols], in_=grouped[:])
-            nc.sync.dma_start(out=words_view(out_1[0])[:, cols], in_=y_c[:, cols].bitcast(I32))
+        def quantise_y(half, y):
+            cols = slice(P * half, P * (half + 1))
+            grouped, dst, src = side_by_side(y[:], "x3_grouped")
+            if half == 0:
+                nc.scalar.copy(out=dst, in_=src)
+            else:
+                nc.vector.tensor_copy(out=dst, in_=src)
+            nc.vector.quantize_mx(out=y_codes[:, cols].bitcast(FP8X4), scales=y_scales[:, cols], in_=grouped[:])
+            nc.sync.dma_start(out=as_words(out_1[0])[:, cols], in_=y_codes[:, cols].bitcast(I32))
 
-        stage3(0, 0)
-        stage3(0, 1)
-        quantise_x3(1, 0)
-        stage3(1, 0)
-        x3_high[1] = last.tile([P, 4, P], F32, name="x3_high")
-        for s in range(4, 8):
-            pick2(s, 1)
-        quantise_x3(1, 1)
-        y0 = finish(0)
-        stage3(1, 1)
-        planes(0, y0)
-        y1 = finish(1)
-        planes(1, y1)
-        for q in range(4):
-            queue = nc.sync if q % 2 == 0 else nc.scalar
+        picks_high = pick_high(0)
+        half_banks = []
+        for half in range(2):
+            cols = slice(P * half, P * (half + 1))
+            half_banks.append([psum.tile([P, 4, P], F32, name="bank") for product in range(2)])
+            last_products(0, half_banks[half], x3_low[0][:, cols], x3_low[1][:, cols])
+        codes, scales = quantise_x3(picks_high, False, "x3_high0")
+        last_products(1, half_banks[0], codes[:], scales[:])
+        codes, scales = quantise_x3(pick_high(1), False, "x3_high1")
+        y = link_index(0)
+        last_products(1, half_banks[1], codes[:], scales[:])
+        quantise_y(0, y)
+        quantise_y(1, link_index(1))
+        for g in range(4):
+            queue = nc.sync if g % 2 == 0 else nc.scalar
             queue.dma_start(
-                out=out_2[0, 4 * q : 4 * q + 4, :].bitcast(I32),
-                in_=y_s[32 * q : 32 * q + 4, :].bitcast(I32),
+                out=out_2[0, 4 * g : 4 * g + 4, :].bitcast(I32),
+                in_=y_scales[32 * g : 32 * g + 4, :].bitcast(I32),
             )

import math
from contextlib import ExitStack

import concourse.mybir as mybir

K, H, N, T, S, P1, P2 = 1024, 1024, 512, 4096, 1024, 512, 256
FLOPS = 2 * K * H * S + 2 * H * H * P1 + 2 * 2 * H * N * P2

F32 = mybir.dt.float32
BF16 = mybir.dt.bfloat16
I32 = mybir.dt.int32
U32 = mybir.dt.uint32
U16 = mybir.dt.uint16
U8 = mybir.dt.uint8
FP8X4 = mybir.dt.float8_e4m3fn_x4
FP4X4 = mybir.dt.float4_e2m1fn_x4
ALU = mybir.AluOpType
ACT = mybir.ActivationFunctionType

P = 128
PASS = 512
BANK = 512
LIST = 16
STEP = 0.9
SLICES = [(b, t) for b in range(2) for t in range(4)]

AHEAD = 2
GAINS_ON_VECTOR = 2
SUMS_ON_GPSIMD = 3
MOVES_ON_GPSIMD = 2


def tile_list_die_link_trunk_kernel(
    tc, tab_words, tab_scales, offs, pos1, pos2, w1, phase, gain, w2_words, w2_scales,
    w3, w4_words, w4_scales, base, out_0, out_1, out_2,
):
    nc = tc.nc
    with ExitStack() as ctx:
        lists = ctx.enter_context(tc.tile_pool(name="lists", bufs=1))
        keep = ctx.enter_context(tc.tile_pool(name="keep", bufs=1))
        raws = ctx.enter_context(tc.tile_pool(name="raws", bufs=2))
        ring = ctx.enter_context(tc.tile_pool(name="ring", bufs=3))
        pair = ctx.enter_context(tc.tile_pool(name="pair", bufs=2))
        chain = ctx.enter_context(tc.tile_pool(name="chain", bufs=1))
        psum = ctx.enter_context(tc.psum_pool(name="psum", bufs=8))

        def held(shape, dtype, name):
            return keep.tile(shape, dtype, name=name, align_bytes=64)

        def as_words(dram):
            return dram.rearrange("p n i -> p (n i)").bitcast(I32)

        def load_block(w, a, b):
            raw = raws.tile([P, 4, PASS], F32, name="raw")
            rows = w[PASS * a : PASS * (a + 1), PASS * b : PASS * (b + 1)]
            nc.sync.dma_start(out=raw[:], in_=rows.rearrange("(p i) c -> p i c", i=4))
            return raw

        def quantise_weight(raw, u, on_scalar, grouped, name):
            src = raw[:].rearrange("p i (m u e) -> p u m i e", u=2, e=2)[:, u]
            dst = grouped[:].rearrange("p (e m i) -> p m i e", e=2, i=4)
            if on_scalar:
                nc.scalar.copy(out=dst, in_=src)
            else:
                nc.vector.tensor_copy(out=dst, in_=src)
            codes = held([P, 2 * P], U32, name + "_codes")
            scales = held([P, 2 * P], U8, name + "_scales")
            nc.vector.quantize_mx(out=codes[:].bitcast(FP8X4), scales=scales[:], in_=grouped[:])
            return codes, scales

        def side_by_side(slices, name):
            grouped = pair.tile([P, 4 * slices.shape[2]], BF16, name=name, align_bytes=64)
            dst = grouped[:].rearrange("p (c n t) -> p c t n", n=4, t=4)
            src = slices.rearrange("p t (c n) -> p c t n", n=4)
            return grouped, dst, src

        offs_t = lists.tile([P, S // LIST], U16, name="offs_t")
        pos1_t = lists.tile([P, P1 // LIST], U16, name="pos1_t")
        pos2_t = lists.tile([P, P2 // LIST], U16, name="pos2_t")

        tab_s = held([P, T], U8, "tab_s")
        zero = held([P, 1], F32, "zero")
        nc.vector.memset(tab_s[:, : T // 2].bitcast(I32), 0)
        nc.gpsimd.memset(tab_s[:, T // 2 :].bitcast(I32), 0)
        nc.vector.memset(zero[:], 0.0)
        v_s = [held([P, S], U8, f"v_s{a}") for a in range(2)]
        for a in range(2):
            nc.gpsimd.memset(v_s[a][:].bitcast(I32), 0)

        tab_w = [chain.tile([P, T], U32, name=f"tab_w{a}", tag=f"wide{a}", align_bytes=64) for a in range(2)]
        phase_t = held([P, 2, 4], F32, "phase_t")
        gain_t = held([P, 2, 4], F32, "gain_t")
        nc.sync.dma_start(offs_t[:], offs)
        nc.sync.dma_start(pos2_t[:], pos2)
        nc.sync.dma_start(pos1_t[:], pos1)
        nc.scalar.dma_start(out=phase_t[:], in_=phase.rearrange("(b p t) -> p b t", b=2, t=4))
        nc.scalar.dma_start(out=gain_t[:], in_=gain.rearrange("(b p t) -> p b t", b=2, t=4))
        nc.sync.dma_start(
            out=tab_s[0:P:4, :].bitcast(I32),
            in_=tab_scales.rearrange("a q n -> (a q) n").bitcast(I32),
        )
        w1_raw = {}
        for a in range(2):
            nc.sync.dma_start(out=tab_w[a][:].bitcast(I32), in_=as_words(tab_words[a]))
            w1_raw[a, 0] = load_block(w1, a, 0)
        for a in range(2):
            w1_raw[a, 1] = load_block(w1, a, 1)
        w2_raw = raws.tile([P, 2, H], I32, name="w2_raw", tag="raw")
        nc.sync.dma_start(out=w2_raw[:], in_=w2_words.rearrange("a p n i -> p a (n i)").bitcast(I32))

        silu_zero = held([P, 1], F32, "silu_zero")
        half_pi = held([P, 1], F32, "half_pi")
        nc.scalar.activation(out=silu_zero[:], in_=zero[:], func=ACT.Silu)
        nc.vector.tensor_scalar(out=half_pi[:], in0=silu_zero[:], scalar1=math.pi / 2, scalar2=None, op0=ALU.add)
        z_gain = held([P, 2, 4], F32, "z_gain")
        nc.vector.tensor_scalar(out=z_gain[:], in0=gain_t[:], scalar1=1 / STEP, scalar2=None, op0=ALU.mult)

        spread_s = held([P, S], U8, "spread_s")
        nc.vector.tensor_copy(out=spread_s[:], in_=tab_s[:].indirect(offs_t[:]))
        for a in range(2):
            for g in range(4):
                first = 4 * (16 * a + 4 * g)
                queue = nc.gpsimd if 4 * a + g < MOVES_ON_GPSIMD else nc.scalar
                queue.dma_start(
                    out=v_s[a][32 * g : 32 * g + 4, :].bitcast(I32),
                    in_=spread_s[first : first + 16 : 4, :].bitcast(I32),
                )
        v_w = {}
        for a in range(2):
            for c in range(S // BANK):
                v_w[a, c] = held([P, BANK], U32, f"v_w{a}{c}")
                entries = offs_t[:, BANK // LIST * c : BANK // LIST * (c + 1)]
                nc.vector.tensor_copy(out=v_w[a, c][:], in_=tab_w[a][:].indirect(entries))

        ws_raw = chain.tile([P, H], U8, name="ws_raw", tag="wide1", align_bytes=64)
        nc.gpsimd.memset(ws_raw[:].bitcast(I32), 0)
        for g in range(4):
            nc.sync.dma_start(
                out=ws_raw[32 * g + 4 : 32 * g + 12, :].bitcast(I32),
                in_=w2_scales[:, 4 * g : 4 * g + 4, :].bitcast(I32),
            )
            nc.sync.dma_start(
                out=ws_raw[32 * g : 32 * g + 4, :].bitcast(I32).rearrange("r (a c) -> r a c", a=2),
                in_=w4_scales[:, 4 * g : 4 * g + 4, :].bitcast(I32).rearrange("a r c -> r a c"),
            )

        z = [held([P, 4, P1], F32, f"z{b}") for b in range(2)]
        x1_codes = [held([P, P1], U32, f"x1_codes{b}") for b in range(2)]
        x1_scales = [held([P, P1], U8, f"x1_scales{b}") for b in range(2)]
        w1_q = {}

        def quantise_w1(a, b, u):
            on_scalar = u == 1 if a == 1 else b == 0
            grouped = ring.tile([P, 2 * PASS], BF16, name="grouped", align_bytes=64)
            w1_q[a, b, u] = quantise_weight(w1_raw[a, b], u, on_scalar, grouped, f"w1_{a}{b}{u}")

        def first_product(b, t):
            u, e = divmod(t, 2)
            angle = ring.tile([P, S], F32, name="angle", bufs=AHEAD + 2)
            for c in range(S // BANK):
                cols = slice(BANK * c, BANK * (c + 1))
                bank = psum.tile([P, BANK], F32, name="bank")
                for a in range(2):
                    codes, scales = w1_q[a, b, u]
                    nc.tensor.matmul_mx(
                        out=bank[:],
                        lhsT=codes[:, P * e : P * (e + 1)].bitcast(FP8X4),
                        lhsT_scale=scales[:, P * e : P * (e + 1)],
                        rhs=v_w[a, c][:].bitcast(FP8X4),
                        rhs_scale=v_s[a][:, cols],
                        start=(a == 0),
                        stop=(a == 1),
                    )
                nc.scalar.activation(out=angle[:, cols], in_=bank[:], func=ACT.Abs, bias=phase_t[:, b, t : t + 1])
            return angle

        def pick_by_pos1(s, angle):
            b, t = SLICES[s]
            is_last = s == len(SLICES) - 1
            width = P1 // 2 if is_last else P1
            pool = chain if is_last else ring
            picked = pool.tile([P, P1], F32, name="picked", align_bytes=64)
            cosine = pool.tile([P, P1], F32, name="cosine", align_bytes=64)
            for c0 in range(0, P1, width):
                entries = pos1_t[:, c0 // LIST : (c0 + width) // LIST]
                nc.vector.tensor_copy(out=picked[:, c0 : c0 + width], in_=angle[:].indirect(entries))
            for c0 in range(0, P1, width):
                cols = slice(c0, c0 + width)
                nc.scalar.activation(
                    out=cosine[:, cols], in_=picked[:, cols], func=ACT.Sin, bias=half_pi[:], scale=-1.0,
                )
                factor = z_gain[:, b, t : t + 1]
                if s < len(SLICES) - GAINS_ON_VECTOR:
                    nc.scalar.activation(out=z[b][:, t, cols], in_=cosine[:, cols], func=ACT.Copy, scale=factor)
                else:
                    nc.vector.tensor_scalar(
                        out=z[b][:, t, cols], in0=cosine[:, cols], scalar1=factor, scalar2=None, op0=ALU.mult,
                    )

        def quantise_x1(b, width):
            groups = []
            for c0 in range(0, P1, width):
                cols = slice(c0, c0 + width)
                grouped, dst, src = side_by_side(z[b][:, :, cols], "x1_grouped")
                nc.vector.tensor_scalar(out=dst, in0=src, scalar1=STEP, scalar2=None, op0=ALU.mult)
                groups.append((cols, grouped))
            for cols, grouped in groups:
                nc.vector.quantize_mx(
                    out=x1_codes[b][:, cols].bitcast(FP8X4), scales=x1_scales[b][:, cols], in_=grouped[:],
                )

        w2_w = [held([P, H], I32, f"w2_w{a}") for a in range(2)]

        def deal_w2(a):
            nc.vector.tensor_copy(
                out=w2_w[a][:].rearrange("p (b t g n) -> p b g t n", b=2, t=4, n=4),
                in_=w2_raw[:, a, :].rearrange("p (b g n t) -> p b g t n", b=2, t=4, n=4),
            )

        for a in range(2):
            for u in range(2):
                quantise_w1(a, 0, u)
        angles = {s: first_product(*SLICES[s]) for s in range(AHEAD)}
        for u in range(2):
            quantise_w1(0, 1, u)
        for s in range(len(SLICES)):
            if s < 2:
                quantise_w1(1, 1, s)
            if s + AHEAD < len(SLICES):
                angles[s + AHEAD] = first_product(*SLICES[s + AHEAD])
            pick_by_pos1(s, angles[s])
            if SLICES[s] == (1, 0):
                quantise_x1(0, P1)
            if SLICES[s] in ((1, 1), (1, 2)):
                deal_w2(SLICES[s][1] - 1)

        w3_raw = [load_block(w3, a, 0) for a in range(2)]
        ws = held([P, H], U8, "ws")
        nc.vector.tensor_copy(
            out=ws[:].rearrange("p (b t m) -> p b t m", b=2, t=4),
            in_=ws_raw[:].rearrange("p (b m t) -> p b t m", b=2, t=4),
        )
        w4_raw = chain.tile([P, 2 * N], U16, name="w4_raw", tag="wide1", align_bytes=64)
        nc.sync.dma_start(
            out=w4_raw[:].bitcast(I32).rearrange("p (a c) -> p a c", a=2),
            in_=w4_words.bitcast(I32).rearrange("a p c -> p a c"),
        )
        w4_w = held([P, 2 * N], U16, "w4_w")
        nc.vector.tensor_copy(
            out=w4_w[:].rearrange("p (a t m) -> p a t m", a=2, t=4),
            in_=w4_raw[:].rearrange("p (a m t) -> p a t m", a=2, t=4),
        )
        base_t = chain.tile([P, 4, P2], F32, name="base_t", tag="wide1", align_bytes=64)
        nc.sync.dma_start(out=base_t[:], in_=base.rearrange("(p t) j -> p t j", t=4))
        quantise_x1(1, P1 // 2)

        stepped = [held([P, P1], F32, f"stepped{s}") for s in range(len(SLICES))]

        def least_of(b, t):
            bank = psum.tile([P, BANK], F32, name="bank")
            cols = slice(PASS * b + P * t, PASS * b + P * (t + 1))
            for a in range(2):
                nc.tensor.matmul_mx(
                    out=bank[:],
                    lhsT=w2_w[a][:, cols].bitcast(FP8X4),
                    lhsT_scale=ws[4 + 4 * a : P, cols],
                    rhs=x1_codes[a][:].bitcast(FP8X4),
                    rhs_scale=x1_scales[a][:],
                    start=(a == 0),
                    stop=(a == 1),
                )
            least = held([P, P1], F32, f"least{b}{t}")
            nc.vector.scalar_tensor_tensor(
                out=least[:], in0=z[b][:, t, :], scalar=STEP, in1=bank[:], op0=ALU.mult, op1=ALU.min,
            )
            return least

        def step(engine, s):
            b, t = SLICES[s]
            engine.tensor_tensor(out=stepped[s][:], in0=leasts[s][:], in1=z[b][:, t, :], op=ALU.add)

        def pick_by_pos2(b, picks, c0):
            width = picks[:].shape[2]
            entries = pos2_t[:, c0 // LIST : (c0 + width) // LIST]
            for t in range(4):
                nc.vector.tensor_copy(out=picks[:, t, :], in_=stepped[4 * b + t][:].indirect(entries))

        def quantise_x3(picks, on_scalar, name):
            width = picks[:].shape[2]
            grouped, dst, src = side_by_side(picks[:], "x3_grouped")
            if on_scalar:
                nc.scalar.activation(out=dst, in_=src, func=ACT.Copy, scale=STEP)
            else:
                nc.vector.tensor_scalar(out=dst, in0=src, scalar1=STEP, scalar2=None, op0=ALU.mult)
            codes = held([P, width], U32, name + "_codes")
            scales = held([P, width], U8, name + "_scales")
            nc.vector.quantize_mx(out=codes[:].bitcast(FP8X4), scales=scales[:], in_=grouped[:])
            return codes, scales

        leasts = [least_of(b, t) for b, t in SLICES]
        for s in range(SUMS_ON_GPSIMD):
            step(nc.gpsimd, s)
        w3_q = {}
        for a in range(2):
            for u in range(2):
                grouped = chain.tile(
                    [P, 2 * PASS], BF16, name="w3_grouped", tag=("picked", "cosine")[u], align_bytes=64,
                )
                w3_q[a, u] = quantise_weight(w3_raw[a], u, True, grouped, f"w3_{a}{u}")

        for s in range(SUMS_ON_GPSIMD, 4):
            step(nc.vector, s)
        picks_low = held([P, 4, P2], F32, "picks_low")
        pick_by_pos2(0, picks_low, 0)
        for s in range(4, 6):
            step(nc.vector, s)
        x3_low = quantise_x3(picks_low, True, "x3_low")
        for s in range(6, 8):
            step(nc.vector, s)

        y_codes = held([P, P2], U32, "y_codes")
        y_scales = held([P, P2], U8, "y_scales")

        def last_products(a, banks, codes, scales):
            f_bank, l_bank = banks
            for t in range(4):
                u, e = divmod(t, 2)
                w_codes, w_scales = w3_q[a, u]
                nc.tensor.matmul_mx(
                    out=f_bank[:, t, :],
                    lhsT=w_codes[:, P * e : P * (e + 1)].bitcast(FP8X4),
                    lhsT_scale=w_scales[:, P * e : P * (e + 1)],
                    rhs=codes.bitcast(FP8X4),
                    rhs_scale=scales,
                    start=(a == 0 and t == 0),
                    stop=(a == 1 and t == 3),
                )
            for t in range(4):
                cols = slice(N * a + P * t, N * a + P * (t + 1))
                nc.tensor.matmul_mx(
                    out=l_bank[:, t, :],
                    lhsT=w4_w[:, cols].bitcast(FP4X4),
                    lhsT_scale=ws[:, cols],
                    rhs=codes.bitcast(FP8X4),
                    rhs_scale=scales,
                    start=(a == 0 and t == 0),
                    stop=(a == 1 and t == 3),
                )

        def pick_high(half):
            picks_high = chain.tile([P, 4, P], F32, name="picks_high")
            pick_by_pos2(1, picks_high, P * half)
            return picks_high

        def link_index(half):
            f_bank, l_bank = half_banks[half]
            cols = slice(P * half, P * (half + 1))
            gate = pair.tile([P, 4, P], F32, name="gate")
            nc.scalar.activation(out=gate[:], in_=f_bank[:], func=ACT.Tanh)
            link = pair.tile([P, 4, P], F32, name="link")
            nc.vector.tensor_tensor(out=link[:], in0=l_bank[:], in1=gate[:], op=ALU.mult)
            y = pair.tile([P, 4, P], F32, name="y")
            nc.vector.tensor_tensor(out=y[:], in0=link[:], in1=base_t[:, :, cols], op=ALU.add)
            nc.sync.dma_start(out=out_0.rearrange("(p t) j -> p t j", t=4)[:, :, cols], in_=y[:])
            return y

        def quantise_y(half, y):
            cols = slice(P * half, P * (half + 1))
            grouped, dst, src = side_by_side(y[:], "x3_grouped")
            if half == 0:
                nc.scalar.copy(out=dst, in_=src)
            else:
                nc.vector.tensor_copy(out=dst, in_=src)
            nc.vector.quantize_mx(out=y_codes[:, cols].bitcast(FP8X4), scales=y_scales[:, cols], in_=grouped[:])
            nc.sync.dma_start(out=as_words(out_1[0])[:, cols], in_=y_codes[:, cols].bitcast(I32))

        picks_high = pick_high(0)
        half_banks = []
        for half in range(2):
            cols = slice(P * half, P * (half + 1))
            half_banks.append([psum.tile([P, 4, P], F32, name="bank") for product in range(2)])
            last_products(0, half_banks[half], x3_low[0][:, cols], x3_low[1][:, cols])
        codes, scales = quantise_x3(picks_high, False, "x3_high0")
        last_products(1, half_banks[0], codes[:], scales[:])
        codes, scales = quantise_x3(pick_high(1), False, "x3_high1")
        y = link_index(0)
        last_products(1, half_banks[1], codes[:], scales[:])
        quantise_y(0, y)
        quantise_y(1, link_index(1))
        for g in range(4):
            queue = nc.sync if g % 2 == 0 else nc.scalar
            queue.dma_start(
                out=out_2[0, 4 * g : 4 * g + 4, :].bitcast(I32),
                in_=y_scales[32 * g : 32 * g + 4, :].bitcast(I32),
            )
